import numpy as np
CORES = [34,162,290,418,42,426]
N = 6
TK = 128
CNT = [48,128,16,112,16,16]
NT = sum(CNT)
EPS = 0.01
def setup_inputs(rng):
    return {"x": rng.standard_normal((N, 128, TK), dtype=np.float32) * (0.5 + np.arange(N, dtype=np.float32).reshape(N, 1, 1) / N) + rng.standard_normal((N, 128, 1), dtype=np.float32)}
def setup_inputs_big(rng):
    d = setup_inputs(rng)
    for k in ("x",): d[k] = (d[k].astype(np.float32) * 1024.0).astype(d[k].dtype)
    return d
def setup_inputs_small(rng):
    d = setup_inputs(rng)
    for k in ("x",): d[k] = (d[k].astype(np.float32) * (1 / 1024.0)).astype(d[k].dtype)
    return d
def setup_inputs_apart(rng):
    d = setup_inputs(rng)
    f = (10.0 ** rng.permutation(np.linspace(-1.5, 1.5, N))).astype(np.float32).reshape(N, 1, 1)
    for k in ("x",): d[k] = (d[k].astype(np.float32) * f).astype(d[k].dtype)
    return d
def setup_inputs_mixed(rng):
    d = setup_inputs(rng)
    f = (10.0 ** rng.uniform(-3, 3, (1, 128, 1))).astype(np.float32); shape = rng.integers(3, size=(1, 128, 1))
    for k in ("x",):
        x = d[k].astype(np.float32)
        m = x.mean(axis=(0, 2), keepdims=True); level = m + np.sign(x - m) * np.abs(x - m).mean(axis=(0, 2), keepdims=True) * rng.uniform(0.9, 1.1, x.shape).astype(np.float32)
        other = x * np.where(rng.random(x.shape) < 0.5, 0.1, 1.0).astype(np.float32)
        d[k] = (np.where(shape == 1, level, np.where(shape == 2, other, x)) * f).astype(d[k].dtype)
    return d
def setup_inputs_offset(rng):
    d = setup_inputs(rng)
    x = d["x"]; spread = x.std(axis=(0, 2), keepdims=True)
    d["x"] = (x + spread * rng.uniform(16, 48, (1, 128, 1)) * rng.choice([-1.0, 1.0], (1, 128, 1))).astype(np.float32)
    return d
def reference(x):
    X = x.astype(np.float64); ok = np.arange(TK).reshape(1, 1, TK) < np.array(CNT).reshape(N, 1, 1)
    mu = (X * ok).sum(axis=(0, 2)).reshape(1, 128, 1) / NT
    rs = 1.0 / np.sqrt((((X - mu) ** 2) * ok).sum(axis=(0, 2)).reshape(1, 128, 1) / NT + EPS)
    return {"y": np.where(ok, (X - mu) * rs, np.nan).astype(np.float32)}

@@ -1,0 +1,184 @@
+import math
+from concourse.bass import DstId, RemoteDMATransfer
+from concourse.mybir import AluOpType, AxisListType, ActivationFunctionType
+
+U_TOT = 42
+U_MAX = 16
+EPS = 0.01
+ENGINES = 8
+
+SCRATCH = {
+    "xs": ("sbuf", [128, 128], "float32"),
+    "sq": ("sbuf", [128, 128], "float32"),
+    "xi": ("sbuf", [128, 128], "float32"),
+    "ys": ("sbuf", [128, 128], "float32"),
+    "land": ("sbuf", [128, 2 * U_TOT + 4], "float32"),
+    "ones": ("sbuf", [128, U_MAX], "float32"),
+    "sm": ("sbuf", [128, 4], "float32"),
+    "fin": ("sbuf", [128, 8], "float32"),
+}
+SEMAPHORES = ["ld", "ini", "s_sum", "s_nm", "s_v", "s_q", "r1", "r2", "sent",
+              "f_r", "f_q", "f_mu", "f_b", "f_v", "f_iv", "f_xi", "f_s", "f_y", "done"]
+
+
+def _subsets(items, k):
+    if k == 0:
+        return [[]]
+    out = []
+    for i in range(len(items) - k + 1):
+        for rest in _subsets(items[i + 1:], k - 1):
+            out.append([items[i]] + rest)
+    return out
+
+
+def _perms(items):
+    if not items:
+        return [[]]
+    out = []
+    for i in range(len(items)):
+        for rest in _perms(items[:i] + items[i + 1:]):
+            out.append([items[i]] + rest)
+    return out
+
+
+def _plan(cores, topo):
+    n = len(cores)
+
+    def both(a, b):
+        return topo.may_write(cores[a], cores[b]) and topo.may_write(cores[b], cores[a])
+
+    best = None
+    for ga in _subsets(list(range(n)), n // 2):
+        if 0 not in ga:
+            continue
+        gb = [r for r in range(n) if r not in ga]
+        if not all(both(a, b) for grp in (ga, gb) for a in grp for b in grp if a < b):
+            continue
+        for pb in _perms(gb):
+            if not all(both(a, b) for a, b in zip(ga, pb)):
+                continue
+            score = sum(1 for a, b in zip(ga, pb) if topo.chip(cores[a]) == topo.chip(cores[b]))
+            if best is None or score > best[0]:
+                best = (score, ga, pb)
+    if best is None:
+        raise ValueError("no two-hop plan for these cores")
+    return best[1], best[2]
+
+
+def _engines(allowed, k):
+    m, left = 0, k
+    for b in range(allowed.bit_length()):
+        if left and (allowed >> b) & 1:
+            m |= 1 << b
+            left -= 1
+    return m, k - left
+
+
+def rank_program(g, core, T, topo):
+    rank = T.rank_of(core)
+    if rank is None:
+        return
+    cores = list(T.cores)
+    cnt = [int(c) for c in T.tables["CNT"]]
+    nt = sum(cnt)
+    gc = 0
+    for c in cnt:
+        gc = math.gcd(gc, c)
+    u = [2 * c // gc for c in cnt]
+    U = sum(u)
+    if U != U_TOT or max(u) > U_MAX:
+        raise ValueError("SCRATCH sizes do not fit CNT")
+
+    ga, gb = _plan(cores, topo)
+    mine, other = (ga, gb) if rank in ga else (gb, ga)
+    pos = mine.index(rank)
+    partner = other[pos]
+    peers = [mine[(pos + k) % len(mine)] for k in range(1, len(mine))]
+    off, o = {}, 0
+    for r in ga + gb:
+        off[r] = o
+        o += 2 * u[r]
+    reg0 = off[mine[0]]
+    reg1 = reg0 + 2 * sum(u[r] for r in mine)
+
+    allowed = topo.mask(core, cores[partner])
+    for p in peers:
+        allowed &= topo.mask(core, cores[p])
+    mask, E = _engines(allowed, ENGINES)
+
+    n, ur, ob = cnt[rank], u[rank], off[rank]
+    sem = T.sem
+    V, S, Y = g.vector, g.scalar, g.sync
+    mult, add, sub = AluOpType.mult, AluOpType.add, AluOpType.subtract
+    X = AxisListType.X
+    x_own = T.xs[:, 0:n]
+    blk = T.land[:, ob:ob + 2 * ur]
+    m_all = T.land[:, 0:2 * U:2]
+    q_all = T.land[:, 1:2 * U + 2:4]
+    a_all = T.land[:, 3:2 * U:4]
+    fS, fNM = T.sm[:, 0:1], T.sm[:, 1:2]
+    fR, fQ, fMU, fB, fV, fIV, fSQ = [T.fin[:, k:k + 1] for k in range(7)]
+
+    Y.dma_start(x_own, T.x[:, 0:n]).then_inc(sem.ld, 16)
+    V.memset(T.ones[:, 0:ur], 1.0).then_inc(sem.ini, 1)
+    V.memset(blk, 0.0).then_inc(sem.ini, 1)
+    V.memset(T.land[:, 2 * U:2 * U + 4], EPS).then_inc(sem.ini, 1)
+
+    V.wait_ge(sem.ini, 3)
+    V.wait_ge(sem.ld, 16)
+    V.tensor_reduce(fS, x_own, X, add).then_inc(sem.s_sum, 1)
+    V.wait_ge(sem.s_sum, 1)
+    V.tensor_scalar(fNM, fS, -1.0 / (n * math.sqrt(nt)), None, mult).then_inc(sem.s_nm, 1)
+    V.tensor_scalar(T.land[:, ob:ob + 2 * ur:2], T.ones[:, 0:ur], fS, U ** -1.5 / n, mult, mult).then_inc(sem.s_v, 1)
+    V.tensor_scalar(T.land[:, ob + 3:ob + 4], fS, 1.0 / (nt * math.sqrt(U)), None, mult).then_inc(sem.s_v, 1)
+    S.wait_ge(sem.ini, 3)
+    S.wait_ge(sem.ld, 16)
+    S.wait_ge(sem.s_nm, 1)
+    S.activation(T.sq[:, 0:n], x_own, ActivationFunctionType.Square, bias=fNM, scale=1.0 / math.sqrt(nt),
+                 accum_out=T.land[:, ob + 1:ob + 2]).then_inc(sem.s_q, 1)
+
+    g.wait_ge(sem.ini, 3)
+    g.wait_ge(sem.s_v, 2)
+    g.wait_ge(sem.s_q, 1)
+    ids = []
+    for p in peers:
+        rid, pid = topo.addr(cores[p], core)
+        ids.append(DstId(rid=rid, pnc=pid))
+    g.remote_dma_fused([RemoteDMATransfer(dst_ids=ids, dma_engine_mask=mask, remote_sem=sem.r1,
+                                          srcs=[blk], dsts=[blk for _ in peers])], local_sem=sem.sent)
+    g.wait_ge(sem.r1, E * len(peers))
+    rid, pid = topo.addr(cores[partner], core)
+    region = T.land[:, reg0:reg1]
+    g.remote_dma(region, region, sem.r2, sem.sent, pid, rid, mask)
+
+    for q in (V, S):
+        q.wait_ge(sem.s_v, 2)
+        q.wait_ge(sem.s_q, 1)
+        q.wait_ge(sem.r1, E * len(peers))
+        q.wait_ge(sem.r2, E)
+    V.tensor_reduce(fR, a_all, X, add).then_inc(sem.f_r, 1)
+    V.tensor_reduce(fQ, q_all, X, add).then_inc(sem.f_q, 1)
+    S.wait_ge(sem.f_r, 1)
+    S.activation(T.sq[:, 0:U], m_all, ActivationFunctionType.Square, bias=fR, scale=-float(U),
+                 accum_out=fB).then_inc(sem.f_b, 1)
+    S.wait_ge(sem.f_b, 1)
+    S.wait_ge(sem.f_q, 1)
+    S.activation(fSQ, fB, ActivationFunctionType.Sqrt, bias=fQ, scale=1.0).then_inc(sem.f_s, 1)
+    V.wait_ge(sem.f_r, 1)
+    V.tensor_scalar(fMU, fR, math.sqrt(U), None, mult).then_inc(sem.f_mu, 1)
+    V.wait_ge(sem.f_q, 1)
+    V.wait_ge(sem.f_b, 1)
+    V.tensor_tensor(fV, fB, fQ, add).then_inc(sem.f_v, 1)
+    V.wait_ge(sem.f_v, 1)
+    V.reciprocal(fIV, fV).then_inc(sem.f_iv, 1)
+    V.wait_ge(sem.f_iv, 1)
+    V.wait_ge(sem.f_mu, 1)
+    V.tensor_scalar(T.xi[:, 0:n], x_own, fMU, fIV, sub, mult).then_inc(sem.f_xi, 1)
+    V.wait_ge(sem.f_xi, 1)
+    V.wait_ge(sem.f_s, 1)
+    V.tensor_scalar(T.ys[:, 0:n], T.xi[:, 0:n], fSQ, None, mult).then_inc(sem.f_y, 1)
+
+    Y.wait_ge(sem.f_y, 1)
+    Y.dma_start(T.y[:, 0:n], T.ys[:, 0:n]).then_inc(sem.done, 16)
+    Y.wait_ge(sem.done, 16)
+    g.wait_ge(sem.sent, 2 * E)

@@ -2,8 +2,8 @@ import math
 from concourse.bass import DstId, RemoteDMATransfer
 from concourse.mybir import AluOpType, AxisListType, ActivationFunctionType
 
-U_TOT = 42
-U_MAX = 16
+N_RANKS = 6
+BW = 4
 EPS = 0.01
 ENGINES = 8
 
@@ -12,13 +12,18 @@ SCRATCH = {
     "sq": ("sbuf", [128, 128], "float32"),
     "xi": ("sbuf", [128, 128], "float32"),
     "ys": ("sbuf", [128, 128], "float32"),
-    "land": ("sbuf", [128, 2 * U_TOT + 4], "float32"),
-    "ones": ("sbuf", [128, U_MAX], "float32"),
-    "sm": ("sbuf", [128, 4], "float32"),
-    "fin": ("sbuf", [128, 8], "float32"),
+    "land": ("sbuf", [128, BW * (N_RANKS + 1)], "float32"),
+    "ctab": ("sbuf", [128, 2], "float32"),
+    "cw": ("sbuf", [128, N_RANKS], "float32"),
+    "cq": ("sbuf", [128, N_RANKS + 1], "float32"),
+    "ktab": ("sbuf", [128, N_RANKS], "float32"),
+    "uu": ("sbuf", [128, N_RANKS], "float32"),
+    "sc": ("sbuf", [128, N_RANKS + 1], "float32"),
+    "jk": ("sbuf", [128, 16], "float32"),
+    "fin": ("sbuf", [128, 12], "float32"),
 }
-SEMAPHORES = ["ld", "ini", "s_sum", "s_nm", "s_v", "s_q", "r1", "r2", "sent",
-              "f_r", "f_q", "f_mu", "f_b", "f_v", "f_iv", "f_xi", "f_s", "f_y", "done"]
+SEMAPHORES = ["ld", "ini", "s_sum", "s_v", "s_q", "r1", "r2", "sent", "tb", "w1", "w2",
+              "f_u", "f_q", "f_ra", "f_d", "f_b", "f_x", "f_s", "f_v", "f_iv", "f_xi", "f_y", "done"]
 
 
 def _subsets(items, k):
@@ -81,64 +86,54 @@ def rank_program(g, core, T, topo):
     cores = list(T.cores)
     cnt = [int(c) for c in T.tables["CNT"]]
     nt = sum(cnt)
-    gc = 0
-    for c in cnt:
-        gc = math.gcd(gc, c)
-    u = [2 * c // gc for c in cnt]
-    U = sum(u)
-    if U != U_TOT or max(u) > U_MAX:
-        raise ValueError("SCRATCH sizes do not fit CNT")
+    N = len(cores)
+    if N != N_RANKS:
+        raise ValueError("SCRATCH sizes do not fit the group")
 
     ga, gb = _plan(cores, topo)
+    order = ga + gb
     mine, other = (ga, gb) if rank in ga else (gb, ga)
     pos = mine.index(rank)
     partner = other[pos]
     peers = [mine[(pos + k) % len(mine)] for k in range(1, len(mine))]
-    off, o = {}, 0
-    for r in ga + gb:
-        off[r] = o
-        o += 2 * u[r]
-    reg0 = off[mine[0]]
-    reg1 = reg0 + 2 * sum(u[r] for r in mine)
+    reg0 = BW * order.index(mine[0])
+    reg1 = reg0 + BW * len(mine)
+    n_grp = sum(cnt[r] for r in mine)
 
     allowed = topo.mask(core, cores[partner])
     for p in peers:
         allowed &= topo.mask(core, cores[p])
     mask, E = _engines(allowed, ENGINES)
 
-    n, ur, ob = cnt[rank], u[rank], off[rank]
+    n, ob, W = cnt[rank], BW * order.index(rank), BW * N
     sem = T.sem
     V, S, Y = g.vector, g.scalar, g.sync
     mult, add, sub = AluOpType.mult, AluOpType.add, AluOpType.subtract
     X = AxisListType.X
+    AF = ActivationFunctionType
     x_own = T.xs[:, 0:n]
-    blk = T.land[:, ob:ob + 2 * ur]
-    m_all = T.land[:, 0:2 * U:2]
-    q_all = T.land[:, 1:2 * U + 2:4]
-    a_all = T.land[:, 3:2 * U:4]
-    fS, fNM = T.sm[:, 0:1], T.sm[:, 1:2]
-    fR, fQ, fMU, fB, fV, fIV, fSQ = [T.fin[:, k:k + 1] for k in range(7)]
+    blk = T.land[:, ob:ob + BW]
+    fNS, fSG, fMU, fD, fB, fX, fV, fIV, fSQ = [T.fin[:, k:k + 1] for k in range(9)]
 
     Y.dma_start(x_own, T.x[:, 0:n]).then_inc(sem.ld, 16)
-    V.memset(T.ones[:, 0:ur], 1.0).then_inc(sem.ini, 1)
     V.memset(blk, 0.0).then_inc(sem.ini, 1)
-    V.memset(T.land[:, 2 * U:2 * U + 4], EPS).then_inc(sem.ini, 1)
+    V.memset(T.land[:, W:W + BW], 0.0).then_inc(sem.ini, 1)
+    V.memset(T.ctab[:, 0:1], -1.0 / math.sqrt(n * nt)).then_inc(sem.ini, 1)
+    V.memset(T.ctab[:, 1:2], -1.0 / nt).then_inc(sem.ini, 1)
 
-    V.wait_ge(sem.ini, 3)
+    V.wait_ge(sem.ini, 4)
     V.wait_ge(sem.ld, 16)
-    V.tensor_reduce(fS, x_own, X, add).then_inc(sem.s_sum, 1)
+    V.tensor_reduce(fNS, x_own, X, add, negate=True).then_inc(sem.s_sum, 1)
     V.wait_ge(sem.s_sum, 1)
-    V.tensor_scalar(fNM, fS, -1.0 / (n * math.sqrt(nt)), None, mult).then_inc(sem.s_nm, 1)
-    V.tensor_scalar(T.land[:, ob:ob + 2 * ur:2], T.ones[:, 0:ur], fS, U ** -1.5 / n, mult, mult).then_inc(sem.s_v, 1)
-    V.tensor_scalar(T.land[:, ob + 3:ob + 4], fS, 1.0 / (nt * math.sqrt(U)), None, mult).then_inc(sem.s_v, 1)
-    S.wait_ge(sem.ini, 3)
+    V.tensor_scalar(T.land[:, ob:ob + BW:2], T.ctab[:, 0:2], fNS, None, mult).then_inc(sem.s_v, 1)
+    S.wait_ge(sem.ini, 4)
     S.wait_ge(sem.ld, 16)
-    S.wait_ge(sem.s_nm, 1)
-    S.activation(T.sq[:, 0:n], x_own, ActivationFunctionType.Square, bias=fNM, scale=1.0 / math.sqrt(nt),
+    S.wait_ge(sem.s_sum, 1)
+    S.activation(T.sq[:, 0:n], x_own, AF.Square, bias=fNS, scale=float(n),
                  accum_out=T.land[:, ob + 1:ob + 2]).then_inc(sem.s_q, 1)
 
-    g.wait_ge(sem.ini, 3)
-    g.wait_ge(sem.s_v, 2)
+    g.wait_ge(sem.ini, 4)
+    g.wait_ge(sem.s_v, 1)
     g.wait_ge(sem.s_q, 1)
     ids = []
     for p in peers:
@@ -151,28 +146,45 @@ def rank_program(g, core, T, topo):
     region = T.land[:, reg0:reg1]
     g.remote_dma(region, region, sem.r2, sem.sent, pid, rid, mask)
 
+    for t, r in enumerate(order):
+        V.memset(T.cw[:, t:t + 1], math.sqrt(cnt[r] / nt) * nt / n_grp).then_inc(sem.tb, 1)
+        c = 1.0 if t == 0 else (cnt[r] / cnt[order[t - 1]]) ** 2
+        V.memset(T.cq[:, t:t + 1], c).then_inc(sem.tb, 1)
+    V.memset(T.cq[:, N:N + 1], 1.0 / (cnt[order[-1]] ** 2 * nt)).then_inc(sem.tb, 1)
+    V.wait_ge(sem.tb, 2 * N + 1)
+    V.wait_ge(sem.s_v, 1)
+    V.wait_ge(sem.r1, E * len(peers))
+    V.tensor_reduce(fSG, T.land[:, reg0 + 2:reg1:BW], X, add).then_inc(sem.w1, 1)
+    V.wait_ge(sem.w1, 1)
+    V.tensor_scalar(T.ktab[:, 0:N], T.cw[:, 0:N], fSG, None, mult).then_inc(sem.w2, 1)
+    V.tensor_scalar(T.land[:, W + 2:W + 3], fSG, -float(nt) / n_grp, None, mult).then_inc(sem.w2, 1)
+
     for q in (V, S):
-        q.wait_ge(sem.s_v, 2)
+        q.wait_ge(sem.w2, 2)
+        q.wait_ge(sem.s_v, 1)
         q.wait_ge(sem.s_q, 1)
         q.wait_ge(sem.r1, E * len(peers))
         q.wait_ge(sem.r2, E)
-    V.tensor_reduce(fR, a_all, X, add).then_inc(sem.f_r, 1)
-    V.tensor_reduce(fQ, q_all, X, add).then_inc(sem.f_q, 1)
-    S.wait_ge(sem.f_r, 1)
-    S.activation(T.sq[:, 0:U], m_all, ActivationFunctionType.Square, bias=fR, scale=-float(U),
-                 accum_out=fB).then_inc(sem.f_b, 1)
-    S.wait_ge(sem.f_b, 1)
-    S.wait_ge(sem.f_q, 1)
-    S.activation(fSQ, fB, ActivationFunctionType.Sqrt, bias=fQ, scale=1.0).then_inc(sem.f_s, 1)
-    V.wait_ge(sem.f_r, 1)
-    V.tensor_scalar(fMU, fR, math.sqrt(U), None, mult).then_inc(sem.f_mu, 1)
+    V.tensor_tensor(T.uu[:, 0:N], T.land[:, 0:W:BW], T.ktab[:, 0:N], sub).then_inc(sem.f_u, 1)
+    V.tensor_tensor_scan(T.sc[:, 0:N + 1], T.cq[:, 0:N + 1], T.land[:, 1:W + BW:BW], EPS * cnt[order[0]] ** 2 * nt,
+                         mult, add).then_inc(sem.f_q, 1)
+    V.tensor_reduce(fMU, T.land[:, 2:W:BW], X, add).then_inc(sem.f_ra, 1)
+    S.activation(T.jk[:, 0:N + 1], T.land[:, 2:W + BW:BW], AF.Identity, accum_out=fD).then_inc(sem.f_d, 1)
+    S.wait_ge(sem.f_u, 1)
+    S.activation(T.jk[:, 8:8 + N], T.uu[:, 0:N], AF.Square, accum_out=fB).then_inc(sem.f_b, 1)
     V.wait_ge(sem.f_q, 1)
+    V.wait_ge(sem.f_d, 1)
+    V.tensor_scalar(fX, fD, fD, T.sc[:, N:N + 1], mult, sub).then_inc(sem.f_x, 1)
+    S.wait_ge(sem.f_b, 1)
+    S.wait_ge(sem.f_x, 1)
+    S.activation(fSQ, fX, AF.Sqrt, bias=fB, scale=-1.0).then_inc(sem.f_s, 1)
+    V.wait_ge(sem.f_x, 1)
     V.wait_ge(sem.f_b, 1)
-    V.tensor_tensor(fV, fB, fQ, add).then_inc(sem.f_v, 1)
+    V.tensor_tensor(fV, fB, fX, sub).then_inc(sem.f_v, 1)
     V.wait_ge(sem.f_v, 1)
     V.reciprocal(fIV, fV).then_inc(sem.f_iv, 1)
     V.wait_ge(sem.f_iv, 1)
-    V.wait_ge(sem.f_mu, 1)
+    V.wait_ge(sem.f_ra, 1)
     V.tensor_scalar(T.xi[:, 0:n], x_own, fMU, fIV, sub, mult).then_inc(sem.f_xi, 1)
     V.wait_ge(sem.f_xi, 1)
     V.wait_ge(sem.f_s, 1)

@@ -10,7 +10,7 @@ ENGINES = 8
 SCRATCH = {
     "xs": ("sbuf", [128, 128], "float32"),
     "sq": ("sbuf", [128, 128], "float32"),
-    "xi": ("sbuf", [128, 128], "float32"),
+    "xr": ("sbuf", [128, 128], "float32"),
     "ys": ("sbuf", [128, 128], "float32"),
     "land": ("sbuf", [128, BW * (N_RANKS + 1)], "float32"),
     "ctab": ("sbuf", [128, 2], "float32"),
@@ -23,7 +23,7 @@ SCRATCH = {
     "fin": ("sbuf", [128, 12], "float32"),
 }
 SEMAPHORES = ["ld", "ini", "s_sum", "s_v", "s_q", "r1", "r2", "sent", "tb", "w1", "w2",
-              "f_u", "f_q", "f_ra", "f_d", "f_b", "f_x", "f_s", "f_v", "f_iv", "f_xi", "f_y", "done"]
+              "a_s", "a_g", "a_c", "a_x", "f_u", "f_q", "f_d", "f_b", "f_x", "f_mu", "f_s", "f_it", "f_y", "done"]
 
 
 def _subsets(items, k):
@@ -113,7 +113,7 @@ def rank_program(g, core, T, topo):
     AF = ActivationFunctionType
     x_own = T.xs[:, 0:n]
     blk = T.land[:, ob:ob + BW]
-    fNS, fSG, fMU, fD, fB, fX, fV, fIV, fSQ = [T.fin[:, k:k + 1] for k in range(9)]
+    fNS, fSG, fMU, fD, fB, fX, fSA, fG, fKG, fT, fIT = [T.fin[:, k:k + 1] for k in range(11)]
 
     Y.dma_start(x_own, T.x[:, 0:n]).then_inc(sem.ld, 16)
     V.memset(blk, 0.0).then_inc(sem.ini, 1)
@@ -131,6 +131,11 @@ def rank_program(g, core, T, topo):
     S.wait_ge(sem.s_sum, 1)
     S.activation(T.sq[:, 0:n], x_own, AF.Square, bias=fNS, scale=float(n),
                  accum_out=T.land[:, ob + 1:ob + 2]).then_inc(sem.s_q, 1)
+
+    S.wait_ge(sem.s_q, 1)
+    S.activation(fSA, T.land[:, ob + 1:ob + 2], AF.Sqrt, bias=EPS, scale=1.0 / (float(n) * n * nt)).then_inc(sem.a_s, 1)
+    S.wait_ge(sem.a_g, 1)
+    S.activation(T.xr[:, 0:n], x_own, AF.Identity, scale=fG).then_inc(sem.a_x, 1)
 
     g.wait_ge(sem.ini, 4)
     g.wait_ge(sem.s_v, 1)
@@ -150,17 +155,22 @@ def rank_program(g, core, T, topo):
         V.memset(T.cw[:, t:t + 1], math.sqrt(cnt[r] / nt) * nt / n_grp).then_inc(sem.tb, 1)
         c = 1.0 if t == 0 else (cnt[r] / cnt[order[t - 1]]) ** 2
         V.memset(T.cq[:, t:t + 1], c).then_inc(sem.tb, 1)
-    V.memset(T.cq[:, N:N + 1], 1.0 / (cnt[order[-1]] ** 2 * nt)).then_inc(sem.tb, 1)
-    V.wait_ge(sem.tb, 2 * N + 1)
+    V.wait_ge(sem.a_s, 1)
+    V.reciprocal(fG, fSA).then_inc(sem.a_g, 1)
+    V.wait_ge(sem.a_g, 1)
+    V.tensor_scalar(T.cq[:, N:N + 1], fG, fG, 1.0 / (float(cnt[order[-1]]) ** 2 * nt), mult, mult).then_inc(sem.a_c, 1)
+    V.wait_ge(sem.tb, 2 * N)
     V.wait_ge(sem.s_v, 1)
     V.wait_ge(sem.r1, E * len(peers))
     V.tensor_reduce(fSG, T.land[:, reg0 + 2:reg1:BW], X, add).then_inc(sem.w1, 1)
     V.wait_ge(sem.w1, 1)
     V.tensor_scalar(T.ktab[:, 0:N], T.cw[:, 0:N], fSG, None, mult).then_inc(sem.w2, 1)
     V.tensor_scalar(T.land[:, W + 2:W + 3], fSG, -float(nt) / n_grp, None, mult).then_inc(sem.w2, 1)
+    V.tensor_scalar(fKG, fSG, float(nt) / n_grp, fG, mult, mult).then_inc(sem.w2, 1)
 
     for q in (V, S):
-        q.wait_ge(sem.w2, 2)
+        q.wait_ge(sem.w2, 3)
+        q.wait_ge(sem.a_c, 1)
         q.wait_ge(sem.s_v, 1)
         q.wait_ge(sem.s_q, 1)
         q.wait_ge(sem.r1, E * len(peers))
@@ -168,27 +178,22 @@ def rank_program(g, core, T, topo):
     V.tensor_tensor(T.uu[:, 0:N], T.land[:, 0:W:BW], T.ktab[:, 0:N], sub).then_inc(sem.f_u, 1)
     V.tensor_tensor_scan(T.sc[:, 0:N + 1], T.cq[:, 0:N + 1], T.land[:, 1:W + BW:BW], EPS * cnt[order[0]] ** 2 * nt,
                          mult, add).then_inc(sem.f_q, 1)
-    V.tensor_reduce(fMU, T.land[:, 2:W:BW], X, add).then_inc(sem.f_ra, 1)
-    S.activation(T.jk[:, 0:N + 1], T.land[:, 2:W + BW:BW], AF.Identity, accum_out=fD).then_inc(sem.f_d, 1)
+    S.activation(T.jk[:, 0:N + 1], T.land[:, 2:W + BW:BW], AF.Identity, scale=fG, accum_out=fD).then_inc(sem.f_d, 1)
     S.wait_ge(sem.f_u, 1)
-    S.activation(T.jk[:, 8:8 + N], T.uu[:, 0:N], AF.Square, accum_out=fB).then_inc(sem.f_b, 1)
+    S.activation(T.jk[:, 8:8 + N], T.uu[:, 0:N], AF.Square, scale=fG, accum_out=fB).then_inc(sem.f_b, 1)
     V.wait_ge(sem.f_q, 1)
     V.wait_ge(sem.f_d, 1)
     V.tensor_scalar(fX, fD, fD, T.sc[:, N:N + 1], mult, sub).then_inc(sem.f_x, 1)
+    V.tensor_tensor(fMU, fD, fKG, add).then_inc(sem.f_mu, 1)
     S.wait_ge(sem.f_b, 1)
     S.wait_ge(sem.f_x, 1)
-    S.activation(fSQ, fX, AF.Sqrt, bias=fB, scale=-1.0).then_inc(sem.f_s, 1)
-    V.wait_ge(sem.f_x, 1)
-    V.wait_ge(sem.f_b, 1)
-    V.tensor_tensor(fV, fB, fX, sub).then_inc(sem.f_v, 1)
-    V.wait_ge(sem.f_v, 1)
-    V.reciprocal(fIV, fV).then_inc(sem.f_iv, 1)
-    V.wait_ge(sem.f_iv, 1)
-    V.wait_ge(sem.f_ra, 1)
-    V.tensor_scalar(T.xi[:, 0:n], x_own, fMU, fIV, sub, mult).then_inc(sem.f_xi, 1)
-    V.wait_ge(sem.f_xi, 1)
+    S.activation(fT, fX, AF.Sqrt, bias=fB, scale=-1.0).then_inc(sem.f_s, 1)
     V.wait_ge(sem.f_s, 1)
-    V.tensor_scalar(T.ys[:, 0:n], T.xi[:, 0:n], fSQ, None, mult).then_inc(sem.f_y, 1)
+    V.reciprocal(fIT, fT).then_inc(sem.f_it, 1)
+    V.wait_ge(sem.f_it, 1)
+    V.wait_ge(sem.f_mu, 1)
+    V.wait_ge(sem.a_x, 1)
+    V.tensor_scalar(T.ys[:, 0:n], T.xr[:, 0:n], fMU, fIT, sub, mult).then_inc(sem.f_y, 1)
 
     Y.wait_ge(sem.f_y, 1)
     Y.dma_start(T.y[:, 0:n], T.ys[:, 0:n]).then_inc(sem.done, 16)

@@ -4,67 +4,66 @@ from concourse.mybir import AluOpType, AxisListType, ActivationFunctionType
 
 N_RANKS = 6
 BW = 4
+RW = 2 * BW
 EPS = 0.01
 ENGINES = 8
 
 SCRATCH = {
-    "xs": ("sbuf", [128, 128], "float32"),
+    "xs": ("sbuf", [128, 128 + BW], "float32"),
     "sq": ("sbuf", [128, 128], "float32"),
     "xr": ("sbuf", [128, 128], "float32"),
     "ys": ("sbuf", [128, 128], "float32"),
-    "land": ("sbuf", [128, BW * (N_RANKS + 1)], "float32"),
-    "ctab": ("sbuf", [128, 2], "float32"),
-    "cw": ("sbuf", [128, N_RANKS], "float32"),
+    "land": ("sbuf", [128, RW * (N_RANKS + 1)], "float32"),
+    "cw": ("sbuf", [128, 2 * N_RANKS], "float32"),
     "cq": ("sbuf", [128, N_RANKS + 1], "float32"),
-    "ktab": ("sbuf", [128, N_RANKS], "float32"),
-    "uu": ("sbuf", [128, N_RANKS], "float32"),
+    "ktab": ("sbuf", [128, 2 * N_RANKS], "float32"),
+    "uu": ("sbuf", [128, 2 * N_RANKS], "float32"),
     "sc": ("sbuf", [128, N_RANKS + 1], "float32"),
-    "jk": ("sbuf", [128, 16], "float32"),
+    "jk": ("sbuf", [128, 24], "float32"),
     "fin": ("sbuf", [128, 12], "float32"),
 }
-SEMAPHORES = ["ld", "ini", "s_sum", "s_v", "s_q", "r1", "r2", "sent", "tb", "w1", "w2",
-              "a_s", "a_g", "a_c", "a_x", "f_u", "f_q", "f_d", "f_b", "f_x", "f_mu", "f_s", "f_it", "f_y", "done"]
+SEMAPHORES = ["ld", "ini", "s_sum", "s_v", "s_q", "s_t", "r1", "r2", "sent", "tb", "w2",
+              "a_s", "a_g", "a_x", "f_u", "f_q", "f_d", "f_b", "f_x", "f_mu", "f_s", "f_it", "f_y", "done"]
 
 
-def _subsets(items, k):
-    if k == 0:
-        return [[]]
-    out = []
-    for i in range(len(items) - k + 1):
-        for rest in _subsets(items[i + 1:], k - 1):
-            out.append([items[i]] + rest)
-    return out
-
-
-def _perms(items):
+def _pairings(items):
     if not items:
         return [[]]
     out = []
-    for i in range(len(items)):
-        for rest in _perms(items[:i] + items[i + 1:]):
-            out.append([items[i]] + rest)
+    for i in range(1, len(items)):
+        for rest in _pairings(items[1:i] + items[i + 1:]):
+            out.append([(items[0], items[i])] + rest)
     return out
 
 
-def _plan(cores, topo):
-    n = len(cores)
-
+def _plan(cores, cnt, topo):
     def both(a, b):
         return topo.may_write(cores[a], cores[b]) and topo.may_write(cores[b], cores[a])
 
+    def gain(a, b):
+        near = topo.chip(cores[a]) == topo.chip(cores[b]) or topo.mates(cores[a], cores[b])
+        return cnt[a] + cnt[b] if near else 0
+
     best = None
-    for ga in _subsets(list(range(n)), n // 2):
-        if 0 not in ga:
+    for pairs in _pairings(list(range(len(cores)))):
+        if not all(both(a, b) for a, b in pairs):
             continue
-        gb = [r for r in range(n) if r not in ga]
-        if not all(both(a, b) for grp in (ga, gb) for a in grp for b in grp if a < b):
-            continue
-        for pb in _perms(gb):
-            if not all(both(a, b) for a, b in zip(ga, pb)):
-                continue
-            score = sum(1 for a, b in zip(ga, pb) if topo.chip(cores[a]) == topo.chip(cores[b]))
-            if best is None or score > best[0]:
-                best = (score, ga, pb)
+        score, links, ok = sum(gain(a, b) for a, b in pairs), [], True
+        for i in range(len(pairs)):
+            for j in range(i + 1, len(pairs)):
+                P, Q, opt = pairs[i], pairs[j], None
+                for m in ([(P[0], Q[0]), (P[1], Q[1])], [(P[0], Q[1]), (P[1], Q[0])]):
+                    if all(both(a, b) for a, b in m):
+                        s = sum(gain(a, b) for a, b in m)
+                        if opt is None or s > opt[0]:
+                            opt = (s, m)
+                if opt is None:
+                    ok = False
+                else:
+                    score += opt[0]
+                    links += opt[1]
+        if ok and (best is None or score > best[0]):
+            best = (score, pairs, links)
     if best is None:
         raise ValueError("no two-hop plan for these cores")
     return best[1], best[2]
@@ -87,100 +86,109 @@ def rank_program(g, core, T, topo):
     cnt = [int(c) for c in T.tables["CNT"]]
     nt = sum(cnt)
     N = len(cores)
-    if N != N_RANKS:
-        raise ValueError("SCRATCH sizes do not fit the group")
+    if N != N_RANKS or any(c % BW or c < 2 for c in cnt):
+        raise ValueError("SCRATCH sizes or block alignment do not fit the group")
 
-    ga, gb = _plan(cores, topo)
-    order = ga + gb
-    mine, other = (ga, gb) if rank in ga else (gb, ga)
-    pos = mine.index(rank)
-    partner = other[pos]
-    peers = [mine[(pos + k) % len(mine)] for k in range(1, len(mine))]
-    reg0 = BW * order.index(mine[0])
-    reg1 = reg0 + BW * len(mine)
-    n_grp = sum(cnt[r] for r in mine)
+    pairs, links = _plan(cores, cnt, topo)
+    order = [r for p in pairs for r in p]
+    pair = [p for p in pairs if rank in p][0]
+    partner = pair[0] if pair[1] == rank else pair[1]
+    far = [b if a == rank else a for a, b in links if rank in (a, b)]
+    far.sort(key=lambda r: -cnt[r])
+    reg0 = RW * order.index(pair[0])
+    region = T.land[:, reg0:reg0 + 2 * RW]
 
     allowed = topo.mask(core, cores[partner])
-    for p in peers:
+    for p in far:
         allowed &= topo.mask(core, cores[p])
     mask, E = _engines(allowed, ENGINES)
 
-    n, ob, W = cnt[rank], BW * order.index(rank), BW * N
+    n = cnt[rank]
+    nb = n - 1
+    main = [cnt[r] - 1 for r in order]
+    tl = RW * order.index(rank)
+    ob = tl + BW
+    W, NB = RW * N, 2 * N
+    xb = W + BW
     sem = T.sem
     V, S, Y = g.vector, g.scalar, g.sync
     mult, add, sub = AluOpType.mult, AluOpType.add, AluOpType.subtract
     X = AxisListType.X
     AF = ActivationFunctionType
-    x_own = T.xs[:, 0:n]
+    x_own, x_main, x_last = T.xs[:, 0:n], T.xs[:, 0:nb], T.xs[:, nb:n]
+    tail_src = T.xs[:, nb:nb + BW]
+    tail = T.land[:, tl:tl + BW]
     blk = T.land[:, ob:ob + BW]
-    fNS, fSG, fMU, fD, fB, fX, fSA, fG, fKG, fT, fIT = [T.fin[:, k:k + 1] for k in range(11)]
+    fNS, fMU, fD, fB, fX, fSA, fG, fKG, fT, fIT, fG2 = [T.fin[:, k:k + 1] for k in range(11)]
+    rid_p, pid_p = topo.addr(cores[partner], core)
 
     Y.dma_start(x_own, T.x[:, 0:n]).then_inc(sem.ld, 16)
+    V.memset(T.xs[:, n:n + BW], 0.0).then_inc(sem.ini, 1)
     V.memset(blk, 0.0).then_inc(sem.ini, 1)
-    V.memset(T.land[:, W:W + BW], 0.0).then_inc(sem.ini, 1)
-    V.memset(T.ctab[:, 0:1], -1.0 / math.sqrt(n * nt)).then_inc(sem.ini, 1)
-    V.memset(T.ctab[:, 1:2], -1.0 / nt).then_inc(sem.ini, 1)
+    V.memset(T.land[:, xb:xb + BW], 0.0).then_inc(sem.ini, 1)
 
-    V.wait_ge(sem.ini, 4)
+    g.wait_ge(sem.ini, 3)
+    g.wait_ge(sem.ld, 16)
+    g.remote_dma(tail, tail_src, sem.r1, sem.sent, pid_p, rid_p, mask)
+
+    V.wait_ge(sem.ini, 3)
     V.wait_ge(sem.ld, 16)
-    V.tensor_reduce(fNS, x_own, X, add, negate=True).then_inc(sem.s_sum, 1)
+    V.tensor_reduce(fNS, x_main, X, add, negate=True).then_inc(sem.s_sum, 1)
     V.wait_ge(sem.s_sum, 1)
-    V.tensor_scalar(T.land[:, ob:ob + BW:2], T.ctab[:, 0:2], fNS, None, mult).then_inc(sem.s_v, 1)
-    S.wait_ge(sem.ini, 4)
+    V.tensor_scalar(T.land[:, ob:ob + 1], fNS, -1.0 / math.sqrt(nb), None, mult).then_inc(sem.s_v, 1)
+    V.tensor_scalar(T.land[:, ob + 2:ob + 3], fNS, x_last, -1.0 / nt, sub, mult).then_inc(sem.s_v, 1)
+    V.tensor_copy(tail, tail_src).then_inc(sem.s_t, 1)
+    S.wait_ge(sem.ini, 3)
     S.wait_ge(sem.ld, 16)
     S.wait_ge(sem.s_sum, 1)
-    S.activation(T.sq[:, 0:n], x_own, AF.Square, bias=fNS, scale=float(n),
+    S.activation(T.sq[:, 0:nb], x_main, AF.Square, bias=fNS, scale=float(nb),
                  accum_out=T.land[:, ob + 1:ob + 2]).then_inc(sem.s_q, 1)
 
     S.wait_ge(sem.s_q, 1)
-    S.activation(fSA, T.land[:, ob + 1:ob + 2], AF.Sqrt, bias=EPS, scale=1.0 / (float(n) * n * nt)).then_inc(sem.a_s, 1)
+    S.activation(fSA, T.land[:, ob + 1:ob + 2], AF.Sqrt, bias=EPS, scale=1.0 / (float(nb) * nb * nt)).then_inc(sem.a_s, 1)
     S.wait_ge(sem.a_g, 1)
     S.activation(T.xr[:, 0:n], x_own, AF.Identity, scale=fG).then_inc(sem.a_x, 1)
 
-    g.wait_ge(sem.ini, 4)
-    g.wait_ge(sem.s_v, 1)
+    g.wait_ge(sem.s_v, 2)
     g.wait_ge(sem.s_q, 1)
+    g.remote_dma(blk, blk, sem.r1, sem.sent, pid_p, rid_p, mask)
+    g.wait_ge(sem.s_t, 1)
+    g.wait_ge(sem.r1, 2 * E)
     ids = []
-    for p in peers:
+    for p in far:
         rid, pid = topo.addr(cores[p], core)
         ids.append(DstId(rid=rid, pnc=pid))
-    g.remote_dma_fused([RemoteDMATransfer(dst_ids=ids, dma_engine_mask=mask, remote_sem=sem.r1,
-                                          srcs=[blk], dsts=[blk for _ in peers])], local_sem=sem.sent)
-    g.wait_ge(sem.r1, E * len(peers))
-    rid, pid = topo.addr(cores[partner], core)
-    region = T.land[:, reg0:reg1]
-    g.remote_dma(region, region, sem.r2, sem.sent, pid, rid, mask)
+    g.remote_dma_fused([RemoteDMATransfer(dst_ids=ids, dma_engine_mask=mask, remote_sem=sem.r2,
+                                          srcs=[region], dsts=[region for _ in far])], local_sem=sem.sent)
 
-    for t, r in enumerate(order):
-        V.memset(T.cw[:, t:t + 1], math.sqrt(cnt[r] / nt) * nt / n_grp).then_inc(sem.tb, 1)
-        c = 1.0 if t == 0 else (cnt[r] / cnt[order[t - 1]]) ** 2
+    V.memset(T.cw[:, 0:NB:2], -1.0 / nb).then_inc(sem.tb, 1)
+    for t in range(N):
+        V.memset(T.cw[:, 2 * t + 1:2 * t + 2], -math.sqrt(main[t]) / nb).then_inc(sem.tb, 1)
+        c = 1.0 if t == 0 else (main[t] / main[t - 1]) ** 2
         V.memset(T.cq[:, t:t + 1], c).then_inc(sem.tb, 1)
+    V.wait_ge(sem.tb, 2 * N + 1)
+    V.tensor_scalar(T.ktab[:, 0:NB], T.cw[:, 0:NB], fNS, None, mult).then_inc(sem.w2, 1)
+    V.tensor_scalar(T.land[:, xb + 2:xb + 3], fNS, 1.0 / nb, None, mult).then_inc(sem.w2, 1)
     V.wait_ge(sem.a_s, 1)
     V.reciprocal(fG, fSA).then_inc(sem.a_g, 1)
     V.wait_ge(sem.a_g, 1)
-    V.tensor_scalar(T.cq[:, N:N + 1], fG, fG, 1.0 / (float(cnt[order[-1]]) ** 2 * nt), mult, mult).then_inc(sem.a_c, 1)
-    V.wait_ge(sem.tb, 2 * N)
-    V.wait_ge(sem.s_v, 1)
-    V.wait_ge(sem.r1, E * len(peers))
-    V.tensor_reduce(fSG, T.land[:, reg0 + 2:reg1:BW], X, add).then_inc(sem.w1, 1)
-    V.wait_ge(sem.w1, 1)
-    V.tensor_scalar(T.ktab[:, 0:N], T.cw[:, 0:N], fSG, None, mult).then_inc(sem.w2, 1)
-    V.tensor_scalar(T.land[:, W + 2:W + 3], fSG, -float(nt) / n_grp, None, mult).then_inc(sem.w2, 1)
-    V.tensor_scalar(fKG, fSG, float(nt) / n_grp, fG, mult, mult).then_inc(sem.w2, 1)
+    V.tensor_scalar(T.cq[:, N:N + 1], fG, fG, 1.0 / (float(main[-1]) ** 2 * nt), mult, mult).then_inc(sem.w2, 1)
+    V.tensor_scalar(fKG, fNS, -1.0 / nb, fG, mult, mult).then_inc(sem.w2, 1)
+    V.tensor_scalar(fG2, fG, 1.0 / math.sqrt(nt), None, mult).then_inc(sem.w2, 1)
 
     for q in (V, S):
-        q.wait_ge(sem.w2, 3)
-        q.wait_ge(sem.a_c, 1)
-        q.wait_ge(sem.s_v, 1)
+        q.wait_ge(sem.w2, 5)
+        q.wait_ge(sem.s_v, 2)
         q.wait_ge(sem.s_q, 1)
-        q.wait_ge(sem.r1, E * len(peers))
-        q.wait_ge(sem.r2, E)
-    V.tensor_tensor(T.uu[:, 0:N], T.land[:, 0:W:BW], T.ktab[:, 0:N], sub).then_inc(sem.f_u, 1)
-    V.tensor_tensor_scan(T.sc[:, 0:N + 1], T.cq[:, 0:N + 1], T.land[:, 1:W + BW:BW], EPS * cnt[order[0]] ** 2 * nt,
+        q.wait_ge(sem.s_t, 1)
+        q.wait_ge(sem.r1, 2 * E)
+        q.wait_ge(sem.r2, E * len(far))
+    V.tensor_tensor(T.uu[:, 0:NB], T.land[:, 0:W:BW], T.ktab[:, 0:NB], sub).then_inc(sem.f_u, 1)
+    V.tensor_tensor_scan(T.sc[:, 0:N + 1], T.cq[:, 0:N + 1], T.land[:, BW + 1:W + RW:RW], EPS * main[0] ** 2 * nt,
                          mult, add).then_inc(sem.f_q, 1)
-    S.activation(T.jk[:, 0:N + 1], T.land[:, 2:W + BW:BW], AF.Identity, scale=fG, accum_out=fD).then_inc(sem.f_d, 1)
+    S.activation(T.jk[:, 0:N + 1], T.land[:, BW + 2:W + RW:RW], AF.Identity, scale=fG, accum_out=fD).then_inc(sem.f_d, 1)
     S.wait_ge(sem.f_u, 1)
-    S.activation(T.jk[:, 8:8 + N], T.uu[:, 0:N], AF.Square, scale=fG, accum_out=fB).then_inc(sem.f_b, 1)
+    S.activation(T.jk[:, 8:8 + NB], T.uu[:, 0:NB], AF.Square, scale=fG2, accum_out=fB).then_inc(sem.f_b, 1)
     V.wait_ge(sem.f_q, 1)
     V.wait_ge(sem.f_d, 1)
     V.tensor_scalar(fX, fD, fD, T.sc[:, N:N + 1], mult, sub).then_inc(sem.f_x, 1)
@@ -198,4 +206,4 @@ def rank_program(g, core, T, topo):
     Y.wait_ge(sem.f_y, 1)
     Y.dma_start(T.y[:, 0:n], T.ys[:, 0:n]).then_inc(sem.done, 16)
     Y.wait_ge(sem.done, 16)
-    g.wait_ge(sem.sent, 2 * E)
+    g.wait_ge(sem.sent, 3 * E)

import math
from concourse.bass import DstId, RemoteDMATransfer
from concourse.mybir import AluOpType, AxisListType, ActivationFunctionType

N_RANKS = 6
BW = 4
RW = 2 * BW
EPS = 0.01
ENGINES = 8

SCRATCH = {
    "xs": ("sbuf", [128, 128 + BW], "float32"),
    "sq": ("sbuf", [128, 128], "float32"),
    "xr": ("sbuf", [128, 128], "float32"),
    "ys": ("sbuf", [128, 128], "float32"),
    "land": ("sbuf", [128, RW * (N_RANKS + 1)], "float32"),
    "cw": ("sbuf", [128, 2 * N_RANKS], "float32"),
    "cq": ("sbuf", [128, N_RANKS + 1], "float32"),
    "ktab": ("sbuf", [128, 2 * N_RANKS], "float32"),
    "uu": ("sbuf", [128, 2 * N_RANKS], "float32"),
    "sc": ("sbuf", [128, N_RANKS + 1], "float32"),
    "jk": ("sbuf", [128, 24], "float32"),
    "fin": ("sbuf", [128, 12], "float32"),
}
SEMAPHORES = ["ld", "ini", "s_sum", "s_v", "s_q", "s_t", "r1", "r2", "sent", "tb", "w2",
              "a_s", "a_g", "a_x", "f_u", "f_q", "f_d", "f_b", "f_x", "f_mu", "f_s", "f_it", "f_y", "done"]


def _pairings(items):
    if not items:
        return [[]]
    out = []
    for i in range(1, len(items)):
        for rest in _pairings(items[1:i] + items[i + 1:]):
            out.append([(items[0], items[i])] + rest)
    return out


def _plan(cores, cnt, topo):
    def both(a, b):
        return topo.may_write(cores[a], cores[b]) and topo.may_write(cores[b], cores[a])

    def gain(a, b):
        near = topo.chip(cores[a]) == topo.chip(cores[b]) or topo.mates(cores[a], cores[b])
        return cnt[a] + cnt[b] if near else 0

    best = None
    for pairs in _pairings(list(range(len(cores)))):
        if not all(both(a, b) for a, b in pairs):
            continue
        score, links, ok = sum(gain(a, b) for a, b in pairs), [], True
        for i in range(len(pairs)):
            for j in range(i + 1, len(pairs)):
                P, Q, opt = pairs[i], pairs[j], None
                for m in ([(P[0], Q[0]), (P[1], Q[1])], [(P[0], Q[1]), (P[1], Q[0])]):
                    if all(both(a, b) for a, b in m):
                        s = sum(gain(a, b) for a, b in m)
                        if opt is None or s > opt[0]:
                            opt = (s, m)
                if opt is None:
                    ok = False
                else:
                    score += opt[0]
                    links += opt[1]
        if ok and (best is None or score > best[0]):
            best = (score, pairs, links)
    if best is None:
        raise ValueError("no two-hop plan for these cores")
    return best[1], best[2]


def _engines(allowed, k):
    m, left = 0, k
    for b in range(allowed.bit_length()):
        if left and (allowed >> b) & 1:
            m |= 1 << b
            left -= 1
    return m, k - left


def rank_program(g, core, T, topo):
    rank = T.rank_of(core)
    if rank is None:
        return
    cores = list(T.cores)
    cnt = [int(c) for c in T.tables["CNT"]]
    nt = sum(cnt)
    N = len(cores)
    if N != N_RANKS or any(c % BW or c < 2 for c in cnt):
        raise ValueError("SCRATCH sizes or block alignment do not fit the group")

    pairs, links = _plan(cores, cnt, topo)
    order = [r for p in pairs for r in p]
    pair = [p for p in pairs if rank in p][0]
    partner = pair[0] if pair[1] == rank else pair[1]
    far = [b if a == rank else a for a, b in links if rank in (a, b)]
    far.sort(key=lambda r: -cnt[r])
    reg0 = RW * order.index(pair[0])
    region = T.land[:, reg0:reg0 + 2 * RW]

    allowed = topo.mask(core, cores[partner])
    for p in far:
        allowed &= topo.mask(core, cores[p])
    mask, E = _engines(allowed, ENGINES)

    n = cnt[rank]
    nb = n - 1
    main = [cnt[r] - 1 for r in order]
    tl = RW * order.index(rank)
    ob = tl + BW
    W, NB = RW * N, 2 * N
    xb = W + BW
    sem = T.sem
    V, S, Y = g.vector, g.scalar, g.sync
    mult, add, sub = AluOpType.mult, AluOpType.add, AluOpType.subtract
    X = AxisListType.X
    AF = ActivationFunctionType
    x_own, x_main, x_last = T.xs[:, 0:n], T.xs[:, 0:nb], T.xs[:, nb:n]
    tail_src = T.xs[:, nb:nb + BW]
    tail = T.land[:, tl:tl + BW]
    blk = T.land[:, ob:ob + BW]
    fNS, fMU, fD, fB, fX, fSA, fG, fKG, fT, fIT, fG2 = [T.fin[:, k:k + 1] for k in range(11)]
    rid_p, pid_p = topo.addr(cores[partner], core)

    Y.dma_start(x_own, T.x[:, 0:n]).then_inc(sem.ld, 16)
    V.memset(T.xs[:, n:n + BW], 0.0).then_inc(sem.ini, 1)
    V.memset(blk, 0.0).then_inc(sem.ini, 1)
    V.memset(T.land[:, xb:xb + BW], 0.0).then_inc(sem.ini, 1)

    g.wait_ge(sem.ini, 3)
    g.wait_ge(sem.ld, 16)
    g.remote_dma(tail, tail_src, sem.r1, sem.sent, pid_p, rid_p, mask)

    V.wait_ge(sem.ini, 3)
    V.wait_ge(sem.ld, 16)
    V.tensor_reduce(fNS, x_main, X, add, negate=True).then_inc(sem.s_sum, 1)
    V.wait_ge(sem.s_sum, 1)
    V.tensor_scalar(T.land[:, ob:ob + 1], fNS, -1.0 / math.sqrt(nb), None, mult).then_inc(sem.s_v, 1)
    V.tensor_scalar(T.land[:, ob + 2:ob + 3], fNS, x_last, -1.0 / nt, sub, mult).then_inc(sem.s_v, 1)
    V.tensor_copy(tail, tail_src).then_inc(sem.s_t, 1)
    S.wait_ge(sem.ini, 3)
    S.wait_ge(sem.ld, 16)
    S.wait_ge(sem.s_sum, 1)
    S.activation(T.sq[:, 0:nb], x_main, AF.Square, bias=fNS, scale=float(nb),
                 accum_out=T.land[:, ob + 1:ob + 2]).then_inc(sem.s_q, 1)

    S.wait_ge(sem.s_q, 1)
    S.activation(fSA, T.land[:, ob + 1:ob + 2], AF.Sqrt, bias=EPS, scale=1.0 / (float(nb) * nb * nt)).then_inc(sem.a_s, 1)
    S.wait_ge(sem.a_g, 1)
    S.activation(T.xr[:, 0:n], x_own, AF.Identity, scale=fG).then_inc(sem.a_x, 1)

    g.wait_ge(sem.s_v, 2)
    g.wait_ge(sem.s_q, 1)
    g.remote_dma(blk, blk, sem.r1, sem.sent, pid_p, rid_p, mask)
    g.wait_ge(sem.s_t, 1)
    g.wait_ge(sem.r1, 2 * E)
    ids = []
    for p in far:
        rid, pid = topo.addr(cores[p], core)
        ids.append(DstId(rid=rid, pnc=pid))
    g.remote_dma_fused([RemoteDMATransfer(dst_ids=ids, dma_engine_mask=mask, remote_sem=sem.r2,
                                          srcs=[region], dsts=[region for _ in far])], local_sem=sem.sent)

    V.memset(T.cw[:, 0:NB:2], -1.0 / nb).then_inc(sem.tb, 1)
    for t in range(N):
        V.memset(T.cw[:, 2 * t + 1:2 * t + 2], -math.sqrt(main[t]) / nb).then_inc(sem.tb, 1)
        c = 1.0 if t == 0 else (main[t] / main[t - 1]) ** 2
        V.memset(T.cq[:, t:t + 1], c).then_inc(sem.tb, 1)
    V.wait_ge(sem.tb, 2 * N + 1)
    V.tensor_scalar(T.ktab[:, 0:NB], T.cw[:, 0:NB], fNS, None, mult).then_inc(sem.w2, 1)
    V.tensor_scalar(T.land[:, xb + 2:xb + 3], fNS, 1.0 / nb, None, mult).then_inc(sem.w2, 1)
    V.wait_ge(sem.a_s, 1)
    V.reciprocal(fG, fSA).then_inc(sem.a_g, 1)
    V.wait_ge(sem.a_g, 1)
    V.tensor_scalar(T.cq[:, N:N + 1], fG, fG, 1.0 / (float(main[-1]) ** 2 * nt), mult, mult).then_inc(sem.w2, 1)
    V.tensor_scalar(fKG, fNS, -1.0 / nb, fG, mult, mult).then_inc(sem.w2, 1)
    V.tensor_scalar(fG2, fG, 1.0 / math.sqrt(nt), None, mult).then_inc(sem.w2, 1)

    for q in (V, S):
        q.wait_ge(sem.w2, 5)
        q.wait_ge(sem.s_v, 2)
        q.wait_ge(sem.s_q, 1)
        q.wait_ge(sem.s_t, 1)
        q.wait_ge(sem.r1, 2 * E)
        q.wait_ge(sem.r2, E * len(far))
    V.tensor_tensor(T.uu[:, 0:NB], T.land[:, 0:W:BW], T.ktab[:, 0:NB], sub).then_inc(sem.f_u, 1)
    V.tensor_tensor_scan(T.sc[:, 0:N + 1], T.cq[:, 0:N + 1], T.land[:, BW + 1:W + RW:RW], EPS * main[0] ** 2 * nt,
                         mult, add).then_inc(sem.f_q, 1)
    S.activation(T.jk[:, 0:N + 1], T.land[:, BW + 2:W + RW:RW], AF.Identity, scale=fG, accum_out=fD).then_inc(sem.f_d, 1)
    S.wait_ge(sem.f_u, 1)
    S.activation(T.jk[:, 8:8 + NB], T.uu[:, 0:NB], AF.Square, scale=fG2, accum_out=fB).then_inc(sem.f_b, 1)
    V.wait_ge(sem.f_q, 1)
    V.wait_ge(sem.f_d, 1)
    V.tensor_scalar(fX, fD, fD, T.sc[:, N:N + 1], mult, sub).then_inc(sem.f_x, 1)
    V.tensor_tensor(fMU, fD, fKG, add).then_inc(sem.f_mu, 1)
    S.wait_ge(sem.f_b, 1)
    S.wait_ge(sem.f_x, 1)
    S.activation(fT, fX, AF.Sqrt, bias=fB, scale=-1.0).then_inc(sem.f_s, 1)
    V.wait_ge(sem.f_s, 1)
    V.reciprocal(fIT, fT).then_inc(sem.f_it, 1)
    V.wait_ge(sem.f_it, 1)
    V.wait_ge(sem.f_mu, 1)
    V.wait_ge(sem.a_x, 1)
    V.tensor_scalar(T.ys[:, 0:n], T.xr[:, 0:n], fMU, fIT, sub, mult).then_inc(sem.f_y, 1)

    Y.wait_ge(sem.f_y, 1)
    Y.dma_start(T.y[:, 0:n], T.ys[:, 0:n]).then_inc(sem.done, 16)
    Y.wait_ge(sem.done, 16)
    g.wait_ge(sem.sent, 3 * E)
